import numpy as np
import ml_dtypes


def mxq(x, axis, fmt="e4m3"):
    dtype, down = {"e4m3": (ml_dtypes.float8_e4m3fn, 7), "e5m2": (ml_dtypes.float8_e5m2, 14)}[fmt]
    v = np.moveaxis(np.asarray(x, np.float32).astype(ml_dtypes.bfloat16).astype(np.float64), axis, -1)
    blocks = v.reshape(v.shape[:-1] + (-1, 32))
    amax = np.abs(blocks).max(-1, keepdims=True)
    byte = np.maximum(np.where(amax > 0, np.frexp(amax)[1] - 1 + 127, 0) - down, 1)
    scale = np.exp2(byte - 127.0)
    codes = (blocks / scale).astype(np.float32).astype(dtype).astype(np.float64)
    return np.moveaxis((codes * scale).reshape(v.shape), -1, axis)


WIDE = False


def mx_kscale(k):
    if not WIDE:
        return np.ones(k)
    levels = np.array([10, -10, 5, -5, 0])
    if k % 512:
        return np.exp2(np.random.permutation(np.resize(levels, k // 32))).repeat(32)
    a = np.empty((k // 512, 16))
    for p in range(k // 512):
        a[p, :8] = np.random.permutation(np.resize(levels, 8))
        for g in range(8):
            far = levels[np.abs(levels - a[p, g]) >= 10]
            a[p, g + 8] = far[np.random.randint(len(far))]
    return np.exp2(a.ravel()).repeat(32)


def f64(x):
    return np.asarray(x).astype(np.float64)


def striped(idx):
    return np.tile(idx.reshape(-1, 16).T, (8, 1)).astype(np.uint16)


def unstriped(offs):
    return offs[:16].T.reshape(-1).astype(np.int64)


def striped8(idx):
    return np.concatenate([x.reshape(-1, 16).T for x in idx]).astype(np.uint16)


def runs(offs, k):
    lists = np.stack([offs[16 * r : 16 * r + 16].T.reshape(-1) for r in range(8)]).astype(np.int64)
    return lists[np.arange(k) % 512 // 64]


def pack_weight(w):
    k, n = w.shape
    w = f64(np.asarray(w, np.float32).astype(ml_dtypes.bfloat16)).reshape(k // 32, 32, n)
    amax = np.abs(w).max(1)
    byte = np.clip(np.where(amax > 0, np.frexp(amax)[1] - 1 + 127 - 7, 1), 1, 254)
    scaled = (w * np.exp2(127.0 - byte)[:, None, :]).reshape(k, n).astype(np.float32)
    words = np.ascontiguousarray(scaled.reshape(k // 512, 128, 4, n).transpose(0, 1, 3, 2)).astype(ml_dtypes.float8_e4m3fn).view(np.uint8)
    return words, np.ascontiguousarray(byte.astype(np.uint8).reshape(k // 512, 16, n))


def unpack_weight(words, scales):
    g, p, n, _ = words.shape
    vals = np.ascontiguousarray(words).view(ml_dtypes.float8_e4m3fn).astype(np.float64) * np.repeat(np.exp2(scales.astype(np.float64) - 127.0), 8, axis=1)[..., None]
    return vals.transpose(0, 1, 3, 2).reshape(g * 512, n)


def sigmoid(v):
    return 1.0 / (1.0 + np.exp(-np.maximum(v, -700.0)))


K, T, S, N, H = 512, 2048, 512, 512, 512


def setup_inputs():
    n = np.random.standard_normal
    s = mx_kscale(K)[:, None]
    u = mx_kscale(H)
    packed_xT = pack_weight(n((K, T)) * s)
    return {
        "x_words": packed_xT[0],
        "x_scales": packed_xT[1],
        "w1": (n((K, H)) / np.sqrt(K) / s).astype(np.float32),
        "gn": (np.random.uniform(0.5, 1.5, (H, 1)) * u[:, None]).astype(np.float32),
        "w2": (n((H, N)) / np.sqrt(H) / u[:, None]).astype(np.float32),
        "w3": (n((K, N)) / np.sqrt(K) / s).astype(np.float32),
        "offs": striped(np.random.permutation(T)[:S]),
        "n1": striped8(np.stack([np.random.permutation(S) for _ in range(8)])),
        "n2": striped8(np.stack([np.random.permutation(S) for _ in range(8)])),
        "two": striped(np.random.permutation(T)[:S]),
        "n3": striped8(np.stack([np.random.permutation(S) for _ in range(8)])),
        "n4": striped8(np.stack([np.random.permutation(S) for _ in range(8)])),
    }


def reference(x_words, x_scales, w1, gn, w2, w3, offs, n1, n2, two, n3, n4):
    xq = unpack_weight(x_words, x_scales)[:, unstriped(offs)]
    y = mxq(f64(w1), 0, "e4m3").T @ xq
    ex = np.exp(0.5 * y)
    z = f64(gn) * ((2.0 * ex) / (ex + ex[np.arange(H)[:, None], runs(n1, H)] + ex[np.arange(H)[:, None], runs(n2, H)]))
    h = mxq(f64(w2), 0, "e4m3").T @ mxq(z, 0, "e4m3")
    x_two = unpack_weight(x_words, x_scales)[:, unstriped(two)]
    d = mxq(f64(w3), 0, "e4m3").T @ x_two
    return (h + h[np.arange(N)[:, None], runs(n3, N)]) * (sigmoid(d + d[np.arange(N)[:, None], runs(n4, N)]))

@@ -1,0 +1,213 @@
+from contextlib import ExitStack
+
+import concourse.mybir as mybir
+
+K, T, S, N, H = 512, 2048, 512, 512, 512
+FLOPS = 3 * 2 * 512 * 512 * 512
+
+F32 = mybir.dt.float32
+BF16 = mybir.dt.bfloat16
+I32 = mybir.dt.int32
+U32 = mybir.dt.uint32
+U16 = mybir.dt.uint16
+U8 = mybir.dt.uint8
+FP8X4 = mybir.dt.float8_e4m3fn_x4
+ACT = mybir.ActivationFunctionType
+ALU = mybir.AluOpType
+
+P = 128
+PACK = 4
+HALF = S // 2
+LIST_COLS = S // 16
+CHUNK = 128
+VECTOR_PLANES = (0, 1)
+SCALAR_PLANES = (2, 3)
+
+
+def halves():
+    return [(slice(u * HALF, (u + 1) * HALF), slice(u * LIST_COLS // 2, (u + 1) * LIST_COLS // 2)) for u in range(2)]
+
+
+def tile_picked_latetriebshare_none_p_kernel(
+    tc, x_words, x_scales, w1, gn, w2, w3, offs, n1, n2, two, n3, n4, out
+):
+    nc = tc.nc
+    with ExitStack() as ctx:
+        keep = ctx.enter_context(tc.tile_pool(name="keep", bufs=1))
+        psum = ctx.enter_context(tc.psum_pool(name="psum", bufs=1))
+
+        def load_list(src, name):
+            tile = keep.tile([P, LIST_COLS], U16, name=name)
+            nc.sync.dma_start(tile[:], src)
+            return tile
+
+        def load_weight_half(w, u, name):
+            raw = keep.tile([P, PACK, HALF], F32, name=name)
+            nc.sync.dma_start(out=raw[:], in_=w.rearrange("(p j) c -> p j c", j=PACK)[:, :, u * HALF : (u + 1) * HALF])
+            return raw
+
+        def dealt_views(grouped, raw, u):
+            dst = grouped[:].rearrange("p (t u m j) -> p u m j t", t=PACK, u=2, j=PACK)[:, u]
+            src = raw[:].rearrange("p j (m t) -> p m j t", t=PACK)
+            return dst, src
+
+        def mx_tiles(name):
+            codes = keep.tile([P, 512], U32, name=name + "_codes", align_bytes=64)
+            scales = keep.tile([P, 512], U8, name=name + "_scales", align_bytes=64)
+            return codes, scales
+
+        def product(bank, w_mx, t, x_mx, cols):
+            rows = slice(t * P, (t + 1) * P)
+            nc.tensor.matmul_mx(
+                out=bank[:, cols],
+                lhsT=w_mx[0][:, rows].bitcast(FP8X4),
+                lhsT_scale=w_mx[1][:, rows],
+                rhs=x_mx[0][:, cols].bitcast(FP8X4),
+                rhs_scale=x_mx[1][:, cols],
+                start=True,
+                stop=True,
+            )
+
+        scale_table = keep.tile([P, T], U8, name="scale_table", align_bytes=64)
+        nc.gpsimd.memset(scale_table[:].bitcast(I32), 0)
+        for q in range(4):
+            nc.gpsimd.dma_start(
+                out=scale_table[32 * q : 32 * q + 4, :].bitcast(I32),
+                in_=x_scales[0, 4 * q : 4 * q + 4, :].bitcast(I32),
+            )
+        offs_sb = load_list(offs, "offs_sb")
+        two_sb = load_list(two, "two_sb")
+        word_table = keep.tile([P, T], I32, name="word_table", align_bytes=64)
+        nc.sync.dma_start(out=word_table[:], in_=x_words[0].rearrange("p n t -> p (n t)").bitcast(I32))
+        w1_raw = [load_weight_half(w1, u, "w1_raw%d" % u) for u in range(2)]
+        n1_sb = load_list(n1, "n1_sb")
+        n2_sb = load_list(n2, "n2_sb")
+        w3_raw = [load_weight_half(w3, u, "w3_raw%d" % u) for u in range(2)]
+        n4_sb = load_list(n4, "n4_sb")
+        n3_sb = load_list(n3, "n3_sb")
+        gain = keep.tile([P, PACK], F32, name="gain")
+        nc.sync.dma_start(out=gain[:], in_=gn.rearrange("(p t) o -> p (t o)", t=PACK))
+        w2_raw = [load_weight_half(w2, u, "w2_raw%d" % u) for u in range(2)]
+
+        def pick(offsets, name):
+            codes, scales = mx_tiles(name)
+            nc.vector.tensor_copy(codes[:], word_table[:].bitcast(U32).indirect(offsets[:]))
+            nc.vector.tensor_copy(scales[:], scale_table[:].indirect(offsets[:]))
+            return codes, scales
+
+        x_mx = pick(offs_sb, "x_offs")
+
+        w1_bf = keep.tile([P, PACK * H], BF16, name="w1_bf", align_bytes=64)
+        for u in range(2):
+            dst, src = dealt_views(w1_bf, w1_raw[u], u)
+            nc.scalar.copy(dst, src)
+        w1_mx = mx_tiles("w1")
+        y_bank = []
+        for t in range(PACK):
+            nc.vector.quantize_mx(
+                out=w1_mx[0][:, t * P : (t + 1) * P].bitcast(FP8X4),
+                scales=w1_mx[1][:, t * P : (t + 1) * P],
+                in_=w1_bf[:, t * 512 : (t + 1) * 512],
+            )
+            bank = psum.tile([P, S], F32, name="y_bank%d" % t)
+            product(bank, w1_mx, t, x_mx, slice(0, S))
+            y_bank.append(bank)
+
+        x_two_mx = pick(two_sb, "x_two")
+
+        def quantise_weight(raw, name):
+            grouped = keep.tile([P, PACK * 512], BF16, name=name + "_bf", align_bytes=64)
+            for u in range(2):
+                dst, src = dealt_views(grouped, raw[u], u)
+                nc.vector.tensor_copy(dst, src)
+            w_mx = mx_tiles(name)
+            nc.vector.quantize_mx(out=w_mx[0][:].bitcast(FP8X4), scales=w_mx[1][:], in_=grouped[:])
+            return w_mx
+
+        w3_mx = quantise_weight(w3_raw, "w3")
+        d_bank = []
+        for t in range(PACK):
+            bank = psum.tile([P, S], F32, name="dh_bank%d" % t)
+            product(bank, w3_mx, t, x_two_mx, slice(0, S))
+            d_bank.append(bank)
+
+        pair_sum = keep.tile([P, PACK, S], F32, name="pair_sum")
+        ex = {}
+        for t in VECTOR_PLANES:
+            ex[t] = keep.tile([P, S], F32, name="ex%d" % t)
+            nc.scalar.activation(ex[t][:], y_bank[t][:], ACT.Exp, scale=0.5)
+        for t in VECTOR_PLANES:
+            first = keep.tile([P, S], F32, name="ex_n1_%d" % t)
+            for cols, lst in halves():
+                nc.vector.tensor_copy(first[:, cols], ex[t][:].indirect(n1_sb[:, lst]))
+            for cols, lst in halves():
+                nc.vector.tensor_tensor(pair_sum[:, t, cols], ex[t][:].indirect(n2_sb[:, lst]), first[:, cols], ALU.add)
+
+        def scalar_plane(t):
+            half_y = keep.tile([P, S], F32, name="half_y%d" % t)
+            nc.scalar.activation(half_y[:], y_bank[t][:], ACT.Copy, scale=0.5)
+            first = keep.tile([P, S], F32, name="ex_n1_%d" % t)
+            second = keep.tile([P, S], F32, name="ex_n2_%d" % t)
+            for cols, lst in halves():
+                nc.scalar.activation(first[:, cols], half_y[:].indirect(n1_sb[:, lst]), ACT.Exp)
+            for cols, lst in halves():
+                nc.scalar.activation(second[:, cols], half_y[:].indirect(n2_sb[:, lst]), ACT.Exp)
+            nc.vector.tensor_tensor(pair_sum[:, t, :], first[:], second[:], ALU.add)
+
+        scalar_plane(SCALAR_PLANES[0])
+        d_window, d_plain = [], []
+        for t in range(PACK):
+            window = keep.tile([P, S], F32, name="d_window%d" % t)
+            nc.scalar.copy(window[:], d_bank[t][:])
+            plain = keep.tile([P, S], F32, name="d_plain%d" % t)
+            nc.sync.dma_start(out=plain[:], in_=window[:])
+            d_window.append(window)
+            d_plain.append(plain)
+        scalar_plane(SCALAR_PLANES[1])
+
+        log_sum = keep.tile([P, PACK, S], F32, name="log_sum")
+        logit = keep.tile([P, PACK, S], F32, name="logit")
+        for t in range(PACK):
+            nc.scalar.activation(log_sum[:, t, :], pair_sum[:, t, :], ACT.Ln)
+            nc.vector.scalar_tensor_tensor(logit[:, t, :], y_bank[t][:], 0.5, log_sum[:, t, :], ALU.mult, ALU.subtract)
+
+        w2_mx = quantise_weight(w2_raw, "w2")
+
+        z_mx = mx_tiles("z")
+        h_bank = [psum.tile([P, S], F32, name="dh_bank%d" % t) for t in range(PACK)]
+        for c in range(S // CHUNK):
+            cols = slice(c * CHUNK, (c + 1) * CHUNK)
+            share = keep.tile([P, CHUNK, PACK], F32, name="share%d" % c)
+            nc.scalar.activation(share[:], logit[:, :, cols].rearrange("p t j -> p j t"), ACT.Sigmoid)
+            z_bf = keep.tile([P, CHUNK, PACK], BF16, name="z_bf%d" % c, align_bytes=64)
+            nc.vector.scalar_tensor_tensor(
+                z_bf[:], share[:], 2.0, gain[:].unsqueeze(1).to_broadcast([P, CHUNK, PACK]), ALU.mult, ALU.mult
+            )
+            nc.vector.quantize_mx(
+                out=z_mx[0][:, cols].bitcast(FP8X4), scales=z_mx[1][:, cols], in_=z_bf[:].rearrange("p j t -> p (j t)")
+            )
+            for t in range(PACK):
+                product(h_bank[t], w2_mx, t, z_mx, cols)
+
+        gate = []
+        for t in range(PACK):
+            d_sum = keep.tile([P, S], F32, name="d_sum%d" % t)
+            for cols, lst in halves():
+                nc.vector.tensor_tensor(d_sum[:, cols], d_window[t][:].indirect(n4_sb[:, lst]), d_plain[t][:, cols], ALU.add)
+            sig = keep.tile([P, S], F32, name="gate%d" % t)
+            nc.scalar.activation(sig[:], d_sum[:], ACT.Sigmoid)
+            gate.append(sig)
+
+        out_rows = out.rearrange("(p t) j -> p t j", t=PACK)
+        for t in range(PACK):
+            window = keep.tile([P, S], F32, name="h_window%d" % t)
+            nc.scalar.copy(window[:], h_bank[t][:])
+            plain = keep.tile([P, S], F32, name="h_plain%d" % t)
+            h_sum = keep.tile([P, S], F32, name="h_sum%d" % t)
+            result = keep.tile([P, S], F32, name="result%d" % t)
+            for cols, lst in halves():
+                nc.scalar.copy(plain[:, cols], h_bank[t][:, cols])
+                nc.vector.tensor_tensor(h_sum[:, cols], window[:].indirect(n3_sb[:, lst]), plain[:, cols], ALU.add)
+            for cols, lst in halves():
+                nc.vector.tensor_tensor(result[:, cols], h_sum[:, cols], gate[t][:, cols], ALU.mult)
+                nc.sync.dma_start(out=out_rows[:, t, cols], in_=result[:, cols])

@@ -20,8 +20,8 @@ PACK = 4
 HALF = S // 2
 LIST_COLS = S // 16
 CHUNK = 128
-VECTOR_PLANES = (0, 1)
-SCALAR_PLANES = (2, 3)
+VECTOR_PLANES = (0,)
+SCALAR_PLANES = (1, 2, 3)
 
 
 def halves():
@@ -41,19 +41,19 @@ def tile_picked_latetriebshare_none_p_kernel(
             nc.sync.dma_start(tile[:], src)
             return tile
 
-        def load_weight_half(w, u, name):
-            raw = keep.tile([P, PACK, HALF], F32, name=name)
+        def load_weight_half(w, u, name, tag):
+            raw = keep.tile([P, PACK, HALF], F32, name=name, tag=tag)
             nc.sync.dma_start(out=raw[:], in_=w.rearrange("(p j) c -> p j c", j=PACK)[:, :, u * HALF : (u + 1) * HALF])
             return raw
 
         def dealt_views(grouped, raw, u):
-            dst = grouped[:].rearrange("p (t u m j) -> p u m j t", t=PACK, u=2, j=PACK)[:, u]
-            src = raw[:].rearrange("p j (m t) -> p m j t", t=PACK)
+            dst = grouped[:].rearrange("p (t u q r j) -> p u q t j r", t=PACK, u=2, r=2, j=PACK)[:, u]
+            src = raw[:].rearrange("p j (q t r) -> p q t j r", t=PACK, r=2)
             return dst, src
 
-        def mx_tiles(name):
-            codes = keep.tile([P, 512], U32, name=name + "_codes", align_bytes=64)
-            scales = keep.tile([P, 512], U8, name=name + "_scales", align_bytes=64)
+        def mx_tiles(name, scale_tag=None):
+            codes = keep.tile([P, 512], U32, name=name + "_codes", tag=name + "_codes", align_bytes=64)
+            scales = keep.tile([P, 512], U8, name=name + "_scales", tag=scale_tag or name + "_scales", align_bytes=64)
             return codes, scales
 
         def product(bank, w_mx, t, x_mx, cols):
@@ -68,36 +68,33 @@ def tile_picked_latetriebshare_none_p_kernel(
                 stop=True,
             )
 
-        scale_table = keep.tile([P, T], U8, name="scale_table", align_bytes=64)
+        scale_table = keep.tile([P, T], U8, name="scale_table", tag="scale_table", align_bytes=64)
         nc.gpsimd.memset(scale_table[:].bitcast(I32), 0)
+        offs_sb = load_list(offs, "offs_sb")
+        word_table = keep.tile([P, T], I32, name="word_table", align_bytes=64)
+        nc.sync.dma_start(out=word_table[:], in_=x_words[0].rearrange("p n t -> p (n t)").bitcast(I32))
         for q in range(4):
-            nc.gpsimd.dma_start(
+            nc.sync.dma_start(
                 out=scale_table[32 * q : 32 * q + 4, :].bitcast(I32),
                 in_=x_scales[0, 4 * q : 4 * q + 4, :].bitcast(I32),
             )
-        offs_sb = load_list(offs, "offs_sb")
         two_sb = load_list(two, "two_sb")
-        word_table = keep.tile([P, T], I32, name="word_table", align_bytes=64)
-        nc.sync.dma_start(out=word_table[:], in_=x_words[0].rearrange("p n t -> p (n t)").bitcast(I32))
-        w1_raw = [load_weight_half(w1, u, "w1_raw%d" % u) for u in range(2)]
+        w1_raw = [load_weight_half(w1, u, "w1_raw%d" % u, "raw%d" % u) for u in range(2)]
+        w3_raw = [load_weight_half(w3, u, "w3_raw%d" % u, "w3_raw%d" % u) for u in range(2)]
         n1_sb = load_list(n1, "n1_sb")
         n2_sb = load_list(n2, "n2_sb")
-        w3_raw = [load_weight_half(w3, u, "w3_raw%d" % u) for u in range(2)]
         n4_sb = load_list(n4, "n4_sb")
         n3_sb = load_list(n3, "n3_sb")
-        gain = keep.tile([P, PACK], F32, name="gain")
-        nc.sync.dma_start(out=gain[:], in_=gn.rearrange("(p t) o -> p (t o)", t=PACK))
-        w2_raw = [load_weight_half(w2, u, "w2_raw%d" % u) for u in range(2)]
 
-        def pick(offsets, name):
-            codes, scales = mx_tiles(name)
+        def pick(offsets, name, scale_tag=None):
+            codes, scales = mx_tiles(name, scale_tag)
             nc.vector.tensor_copy(codes[:], word_table[:].bitcast(U32).indirect(offsets[:]))
             nc.vector.tensor_copy(scales[:], scale_table[:].indirect(offsets[:]))
             return codes, scales
 
         x_mx = pick(offs_sb, "x_offs")
 
-        w1_bf = keep.tile([P, PACK * H], BF16, name="w1_bf", align_bytes=64)
+        w1_bf = keep.tile([P, PACK * H], BF16, name="w1_bf", tag="w_bf", align_bytes=64)
         for u in range(2):
             dst, src = dealt_views(w1_bf, w1_raw[u], u)
             nc.scalar.copy(dst, src)
@@ -113,10 +110,10 @@ def tile_picked_latetriebshare_none_p_kernel(
             product(bank, w1_mx, t, x_mx, slice(0, S))
             y_bank.append(bank)
 
-        x_two_mx = pick(two_sb, "x_two")
+        x_two_mx = pick(two_sb, "x_two", "w_bf")
 
         def quantise_weight(raw, name):
-            grouped = keep.tile([P, PACK * 512], BF16, name=name + "_bf", align_bytes=64)
+            grouped = keep.tile([P, PACK * 512], BF16, name=name + "_bf", tag="scale_table", align_bytes=64)
             for u in range(2):
                 dst, src = dealt_views(grouped, raw[u], u)
                 nc.vector.tensor_copy(dst, src)
@@ -125,36 +122,51 @@ def tile_picked_latetriebshare_none_p_kernel(
             return w_mx
 
         w3_mx = quantise_weight(w3_raw, "w3")
+        gain = keep.tile([P, PACK], F32, name="gain", tag="x_offs_codes", align_bytes=64)
+        gn_rows = gn.rearrange("(q t r) o -> r q (t o)", t=PACK, r=2)
+        with nc.allow_non_contiguous_dma(reason="one gain a feature"):
+            for r in range(2):
+                nc.sync.dma_start(out=gain[r:P:2], in_=gn_rows[r])
+        w2_rows = w2.rearrange("(q t r) c -> r q t c", t=PACK, r=2)
+        w2_raw = []
+        for u in range(2):
+            raw = keep.tile([P, PACK, HALF], F32, name="w2_raw%d" % u, tag="raw%d" % u)
+            for r in range(2):
+                nc.sync.dma_start(out=raw[r:P:2], in_=w2_rows[r][:, :, u * HALF : (u + 1) * HALF])
+            w2_raw.append(raw)
+
         d_bank = []
         for t in range(PACK):
             bank = psum.tile([P, S], F32, name="dh_bank%d" % t)
             product(bank, w3_mx, t, x_two_mx, slice(0, S))
             d_bank.append(bank)
 
-        pair_sum = keep.tile([P, PACK, S], F32, name="pair_sum")
+        pair_sum = keep.tile([P, PACK, S], F32, name="pair_sum", tag="pair_sum")
         ex = {}
         for t in VECTOR_PLANES:
             ex[t] = keep.tile([P, S], F32, name="ex%d" % t)
             nc.scalar.activation(ex[t][:], y_bank[t][:], ACT.Exp, scale=0.5)
+        firsts = keep.tile([P, len(VECTOR_PLANES), S], F32, name="ex_n1_vector", tag="scale_table", align_bytes=64)
         for t in VECTOR_PLANES:
-            first = keep.tile([P, S], F32, name="ex_n1_%d" % t)
+            first = firsts[:, t, :]
             for cols, lst in halves():
                 nc.vector.tensor_copy(first[:, cols], ex[t][:].indirect(n1_sb[:, lst]))
             for cols, lst in halves():
                 nc.vector.tensor_tensor(pair_sum[:, t, cols], ex[t][:].indirect(n2_sb[:, lst]), first[:, cols], ALU.add)
 
         def scalar_plane(t):
-            half_y = keep.tile([P, S], F32, name="half_y%d" % t)
+            half_y = keep.tile([P, S], F32, name="half_y%d" % t, tag="half_y%d" % t)
             nc.scalar.activation(half_y[:], y_bank[t][:], ACT.Copy, scale=0.5)
-            first = keep.tile([P, S], F32, name="ex_n1_%d" % t)
-            second = keep.tile([P, S], F32, name="ex_n2_%d" % t)
+            first = keep.tile([P, S], F32, name="ex_n1_%d" % t, tag="ex_n1_%d" % t)
+            second = keep.tile([P, S], F32, name="ex_n2_%d" % t, tag="ex_n2_%d" % t)
             for cols, lst in halves():
                 nc.scalar.activation(first[:, cols], half_y[:].indirect(n1_sb[:, lst]), ACT.Exp)
             for cols, lst in halves():
                 nc.scalar.activation(second[:, cols], half_y[:].indirect(n2_sb[:, lst]), ACT.Exp)
             nc.vector.tensor_tensor(pair_sum[:, t, :], first[:], second[:], ALU.add)
 
-        scalar_plane(SCALAR_PLANES[0])
+        for t in SCALAR_PLANES[:-1]:
+            scalar_plane(t)
         d_window, d_plain = [], []
         for t in range(PACK):
             window = keep.tile([P, S], F32, name="d_window%d" % t)
@@ -163,9 +175,9 @@ def tile_picked_latetriebshare_none_p_kernel(
             nc.sync.dma_start(out=plain[:], in_=window[:])
             d_window.append(window)
             d_plain.append(plain)
-        scalar_plane(SCALAR_PLANES[1])
+        scalar_plane(SCALAR_PLANES[-1])
 
-        log_sum = keep.tile([P, PACK, S], F32, name="log_sum")
+        log_sum = keep.tile([P, PACK, S], F32, name="log_sum", tag="half_y3")
         logit = keep.tile([P, PACK, S], F32, name="logit")
         for t in range(PACK):
             nc.scalar.activation(log_sum[:, t, :], pair_sum[:, t, :], ACT.Ln)
@@ -178,7 +190,11 @@ def tile_picked_latetriebshare_none_p_kernel(
         for c in range(S // CHUNK):
             cols = slice(c * CHUNK, (c + 1) * CHUNK)
             share = keep.tile([P, CHUNK, PACK], F32, name="share%d" % c)
-            nc.scalar.activation(share[:], logit[:, :, cols].rearrange("p t j -> p j t"), ACT.Sigmoid)
+            nc.scalar.activation(
+                share[:].rearrange("p (a b) t -> p a t b", b=2),
+                logit[:, :, cols].rearrange("p t (a b) -> p a t b", b=2),
+                ACT.Sigmoid,
+            )
             z_bf = keep.tile([P, CHUNK, PACK], BF16, name="z_bf%d" % c, align_bytes=64)
             nc.vector.scalar_tensor_tensor(
                 z_bf[:], share[:], 2.0, gain[:].unsqueeze(1).to_broadcast([P, CHUNK, PACK]), ALU.mult, ALU.mult
@@ -189,16 +205,21 @@ def tile_picked_latetriebshare_none_p_kernel(
             for t in range(PACK):
                 product(h_bank[t], w2_mx, t, z_mx, cols)
 
-        gate = []
+        gate = keep.tile([P, PACK, S], F32, name="gate", tag="pair_sum")
+        late_sums = keep.tile([P, 2, S], F32, name="late_sums", tag="half_y3")
+        d_sums = [
+            keep.tile([P, S], F32, name="d_sum0", tag="ex_n1_3")[:],
+            keep.tile([P, S], F32, name="d_sum1", tag="ex_n2_3")[:],
+            late_sums[:, 0, :],
+            late_sums[:, 1, :],
+        ]
         for t in range(PACK):
-            d_sum = keep.tile([P, S], F32, name="d_sum%d" % t)
+            d_sum = d_sums[t]
             for cols, lst in halves():
                 nc.vector.tensor_tensor(d_sum[:, cols], d_window[t][:].indirect(n4_sb[:, lst]), d_plain[t][:, cols], ALU.add)
-            sig = keep.tile([P, S], F32, name="gate%d" % t)
-            nc.scalar.activation(sig[:], d_sum[:], ACT.Sigmoid)
-            gate.append(sig)
+            nc.scalar.activation(gate[:, t, :], d_sum, ACT.Sigmoid)
 
-        out_rows = out.rearrange("(p t) j -> p t j", t=PACK)
+        out_rows = out.rearrange("(q t r) j -> t q r j", t=PACK, r=2)
         for t in range(PACK):
             window = keep.tile([P, S], F32, name="h_window%d" % t)
             nc.scalar.copy(window[:], h_bank[t][:])
@@ -209,5 +230,5 @@ def tile_picked_latetriebshare_none_p_kernel(
                 nc.scalar.copy(plain[:, cols], h_bank[t][:, cols])
                 nc.vector.tensor_tensor(h_sum[:, cols], window[:].indirect(n3_sb[:, lst]), plain[:, cols], ALU.add)
             for cols, lst in halves():
-                nc.vector.tensor_tensor(result[:, cols], h_sum[:, cols], gate[t][:, cols], ALU.mult)
-                nc.sync.dma_start(out=out_rows[:, t, cols], in_=result[:, cols])
+                nc.vector.tensor_tensor(result[:, cols], h_sum[:, cols], gate[:, t, cols], ALU.mult)
+                nc.sync.dma_start(out=out_rows[t][:, :, cols], in_=result[:, cols])

@@ -1,6 +1,7 @@
 from contextlib import ExitStack
 
 import concourse.mybir as mybir
+from concourse.masks import make_identity
 
 K, T, S, N, H = 512, 2048, 512, 512, 512
 FLOPS = 3 * 2 * 512 * 512 * 512
@@ -20,12 +21,16 @@ PACK = 4
 HALF = S // 2
 LIST_COLS = S // 16
 CHUNK = 128
-VECTOR_PLANES = (0,)
-SCALAR_PLANES = (1, 2, 3)
+LEAD = 64
+VECTOR_PLANES = (0, 1)
+SCALAR_PLANES = (2, 3)
 
 
 def halves():
     return [(slice(u * HALF, (u + 1) * HALF), slice(u * LIST_COLS // 2, (u + 1) * LIST_COLS // 2)) for u in range(2)]
+
+
+WHOLE = [(slice(0, S), slice(0, LIST_COLS))]
 
 
 def tile_picked_latetriebshare_none_p_kernel(
@@ -41,14 +46,14 @@ def tile_picked_latetriebshare_none_p_kernel(
             nc.sync.dma_start(tile[:], src)
             return tile
 
-        def load_weight_half(w, u, name, tag):
-            raw = keep.tile([P, PACK, HALF], F32, name=name, tag=tag)
+        def load_weight_half(w, u, name):
+            raw = keep.tile([P, PACK, HALF], F32, name=name)
             nc.sync.dma_start(out=raw[:], in_=w.rearrange("(p j) c -> p j c", j=PACK)[:, :, u * HALF : (u + 1) * HALF])
-            return raw
+            return raw[:]
 
-        def dealt_views(grouped, raw, u):
-            dst = grouped[:].rearrange("p (t u q r j) -> p u q t j r", t=PACK, u=2, r=2, j=PACK)[:, u]
-            src = raw[:].rearrange("p j (q t r) -> p q t j r", t=PACK, r=2)
+        def dealt_views(grouped, raw, u, parts=2):
+            dst = grouped[:].rearrange("p (t u q r j) -> p u q t j r", t=PACK, u=parts, r=2, j=PACK)[:, u]
+            src = raw.rearrange("p j (q t r) -> p q t j r", t=PACK, r=2)
             return dst, src
 
         def mx_tiles(name, scale_tag=None):
@@ -56,10 +61,10 @@ def tile_picked_latetriebshare_none_p_kernel(
             scales = keep.tile([P, 512], U8, name=name + "_scales", tag=scale_tag or name + "_scales", align_bytes=64)
             return codes, scales
 
-        def product(bank, w_mx, t, x_mx, cols):
+        def product(result, w_mx, t, x_mx, cols):
             rows = slice(t * P, (t + 1) * P)
             nc.tensor.matmul_mx(
-                out=bank[:, cols],
+                out=result,
                 lhsT=w_mx[0][:, rows].bitcast(FP8X4),
                 lhsT_scale=w_mx[1][:, rows],
                 rhs=x_mx[0][:, cols].bitcast(FP8X4),
@@ -68,36 +73,47 @@ def tile_picked_latetriebshare_none_p_kernel(
                 stop=True,
             )
 
-        scale_table = keep.tile([P, T], U8, name="scale_table", tag="scale_table", align_bytes=64)
+        scale_table = keep.tile([P, T], U8, name="scale_table", align_bytes=64)
         nc.gpsimd.memset(scale_table[:].bitcast(I32), 0)
+        identity = keep.tile([P, P], F32, name="identity")
+        make_identity(nc, identity[:])
+        last_window = keep.tile([P, PACK * S], F32, name="last_window")
+        nc.gpsimd.memset(last_window[:, S:], 0.0)
         offs_sb = load_list(offs, "offs_sb")
-        word_table = keep.tile([P, T], I32, name="word_table", align_bytes=64)
-        nc.sync.dma_start(out=word_table[:], in_=x_words[0].rearrange("p n t -> p (n t)").bitcast(I32))
+        two_sb = load_list(two, "two_sb")
         for q in range(4):
             nc.sync.dma_start(
                 out=scale_table[32 * q : 32 * q + 4, :].bitcast(I32),
                 in_=x_scales[0, 4 * q : 4 * q + 4, :].bitcast(I32),
             )
-        two_sb = load_list(two, "two_sb")
-        w1_raw = [load_weight_half(w1, u, "w1_raw%d" % u, "raw%d" % u) for u in range(2)]
-        w3_raw = [load_weight_half(w3, u, "w3_raw%d" % u, "w3_raw%d" % u) for u in range(2)]
+        word_table = keep.tile([P, T], I32, name="word_table", align_bytes=64)
+        nc.sync.dma_start(out=word_table[:], in_=x_words[0].rearrange("p n t -> p (n t)").bitcast(I32))
+        w1_raw = [load_weight_half(w1, u, "w1_raw%d" % u) for u in range(2)]
         n1_sb = load_list(n1, "n1_sb")
         n2_sb = load_list(n2, "n2_sb")
+        w3_raw = [load_weight_half(w3, u, "w3_raw%d" % u) for u in range(2)]
+        w2_rows = w2.rearrange("(q t r) c -> r q t c", t=PACK, r=2)
+        w2_whole = keep.tile([P, PACK, N], F32, name="w2_raw")
+        for r in range(2):
+            nc.sync.dma_start(out=w2_whole[r:P:2], in_=w2_rows[r])
+        w2_raw = [w2_whole[:]]
         n4_sb = load_list(n4, "n4_sb")
         n3_sb = load_list(n3, "n3_sb")
+        gain = keep.tile([P, PACK], F32, name="gain")
+        gn_rows = gn.rearrange("(q t r) o -> r q (t o)", t=PACK, r=2)
+        with nc.allow_non_contiguous_dma(reason="one gain a feature"):
+            for r in range(2):
+                nc.sync.dma_start(out=gain[r:P:2], in_=gn_rows[r])
 
-        def pick(offsets, name, scale_tag=None):
-            codes, scales = mx_tiles(name, scale_tag)
-            nc.vector.tensor_copy(codes[:], word_table[:].bitcast(U32).indirect(offsets[:]))
-            nc.vector.tensor_copy(scales[:], scale_table[:].indirect(offsets[:]))
-            return codes, scales
-
-        x_mx = pick(offs_sb, "x_offs")
+        x_mx, x_two_mx = mx_tiles("x_offs"), mx_tiles("x_two")
+        for picked, offsets in ((x_mx, offs_sb), (x_two_mx, two_sb)):
+            nc.vector.tensor_copy(picked[1][:], scale_table[:].indirect(offsets[:]))
+        for picked, offsets in ((x_mx, offs_sb), (x_two_mx, two_sb)):
+            nc.vector.tensor_copy(picked[0][:], word_table[:].bitcast(U32).indirect(offsets[:]))
 
         w1_bf = keep.tile([P, PACK * H], BF16, name="w1_bf", tag="w_bf", align_bytes=64)
-        for u in range(2):
-            dst, src = dealt_views(w1_bf, w1_raw[u], u)
-            nc.scalar.copy(dst, src)
+        nc.scalar.copy(*dealt_views(w1_bf, w1_raw[0], 0))
+        nc.vector.tensor_copy(*dealt_views(w1_bf, w1_raw[1], 1))
         w1_mx = mx_tiles("w1")
         y_bank = []
         for t in range(PACK):
@@ -106,129 +122,167 @@ def tile_picked_latetriebshare_none_p_kernel(
                 scales=w1_mx[1][:, t * P : (t + 1) * P],
                 in_=w1_bf[:, t * 512 : (t + 1) * 512],
             )
-            bank = psum.tile([P, S], F32, name="y_bank%d" % t)
-            product(bank, w1_mx, t, x_mx, slice(0, S))
-            y_bank.append(bank)
+            if t < 3:
+                bank = psum.tile([P, S], F32, name="y%d" % t, tag="bank%d" % t)
+                product(bank[:], w1_mx, t, x_mx, slice(0, S))
+                y_bank.append(bank)
 
-        x_two_mx = pick(two_sb, "x_two", "w_bf")
 
         def quantise_weight(raw, name):
-            grouped = keep.tile([P, PACK * 512], BF16, name=name + "_bf", tag="scale_table", align_bytes=64)
-            for u in range(2):
-                dst, src = dealt_views(grouped, raw[u], u)
+            grouped = keep.tile([P, PACK * 512], BF16, name=name + "_bf", tag="w_bf", align_bytes=64)
+            for u in range(len(raw)):
+                dst, src = dealt_views(grouped, raw[u], u, len(raw))
                 nc.vector.tensor_copy(dst, src)
             w_mx = mx_tiles(name)
             nc.vector.quantize_mx(out=w_mx[0][:].bitcast(FP8X4), scales=w_mx[1][:], in_=grouped[:])
             return w_mx
 
         w3_mx = quantise_weight(w3_raw, "w3")
-        gain = keep.tile([P, PACK], F32, name="gain", tag="x_offs_codes", align_bytes=64)
-        gn_rows = gn.rearrange("(q t r) o -> r q (t o)", t=PACK, r=2)
-        with nc.allow_non_contiguous_dma(reason="one gain a feature"):
-            for r in range(2):
-                nc.sync.dma_start(out=gain[r:P:2], in_=gn_rows[r])
-        w2_rows = w2.rearrange("(q t r) c -> r q t c", t=PACK, r=2)
-        w2_raw = []
-        for u in range(2):
-            raw = keep.tile([P, PACK, HALF], F32, name="w2_raw%d" % u, tag="raw%d" % u)
-            for r in range(2):
-                nc.sync.dma_start(out=raw[r:P:2], in_=w2_rows[r][:, :, u * HALF : (u + 1) * HALF])
-            w2_raw.append(raw)
-
         d_bank = []
         for t in range(PACK):
-            bank = psum.tile([P, S], F32, name="dh_bank%d" % t)
-            product(bank, w3_mx, t, x_two_mx, slice(0, S))
+            bank = psum.tile([P, S], F32, name="d%d" % t, tag="bank%d" % (3 + t))
+            product(bank[:], w3_mx, t, x_two_mx, slice(0, S))
             d_bank.append(bank)
 
-        pair_sum = keep.tile([P, PACK, S], F32, name="pair_sum", tag="pair_sum")
+        d_window = [keep.tile([P, 2 * S], F32, name="d_window%d" % t) for t in range(PACK)]
+        pair_sum = {}
         ex = {}
         for t in VECTOR_PLANES:
             ex[t] = keep.tile([P, S], F32, name="ex%d" % t)
             nc.scalar.activation(ex[t][:], y_bank[t][:], ACT.Exp, scale=0.5)
-        firsts = keep.tile([P, len(VECTOR_PLANES), S], F32, name="ex_n1_vector", tag="scale_table", align_bytes=64)
+        firsts = keep.tile([P, len(VECTOR_PLANES), S], F32, name="ex_n1_vector", tag="w_bf", align_bytes=64)
         for t in VECTOR_PLANES:
             first = firsts[:, t, :]
+            pair_sum[t] = d_window[2 + t][:, S:]
             for cols, lst in halves():
                 nc.vector.tensor_copy(first[:, cols], ex[t][:].indirect(n1_sb[:, lst]))
             for cols, lst in halves():
-                nc.vector.tensor_tensor(pair_sum[:, t, cols], ex[t][:].indirect(n2_sb[:, lst]), first[:, cols], ALU.add)
+                nc.vector.tensor_tensor(pair_sum[t][:, cols], ex[t][:].indirect(n2_sb[:, lst]), first[:, cols], ALU.add)
 
-        def scalar_plane(t):
-            half_y = keep.tile([P, S], F32, name="half_y%d" % t, tag="half_y%d" % t)
-            nc.scalar.activation(half_y[:], y_bank[t][:], ACT.Copy, scale=0.5)
-            first = keep.tile([P, S], F32, name="ex_n1_%d" % t, tag="ex_n1_%d" % t)
-            second = keep.tile([P, S], F32, name="ex_n2_%d" % t, tag="ex_n2_%d" % t)
-            for cols, lst in halves():
-                nc.scalar.activation(first[:, cols], half_y[:].indirect(n1_sb[:, lst]), ACT.Exp)
-            for cols, lst in halves():
-                nc.scalar.activation(second[:, cols], half_y[:].indirect(n2_sb[:, lst]), ACT.Exp)
-            nc.vector.tensor_tensor(pair_sum[:, t, :], first[:], second[:], ALU.add)
+        half_y = {}
 
-        for t in SCALAR_PLANES[:-1]:
-            scalar_plane(t)
-        d_window, d_plain = [], []
-        for t in range(PACK):
-            window = keep.tile([P, S], F32, name="d_window%d" % t)
-            nc.scalar.copy(window[:], d_bank[t][:])
-            plain = keep.tile([P, S], F32, name="d_plain%d" % t)
-            nc.sync.dma_start(out=plain[:], in_=window[:])
-            d_window.append(window)
-            d_plain.append(plain)
-        scalar_plane(SCALAR_PLANES[-1])
+        def scalar_gathers(t, bank_tag, window, pieces, pair):
+            half_y[t] = window[:, 0:S]
+            nc.scalar.activation(half_y[t], y_bank[t][:], ACT.Copy, scale=0.5)
+            turned_sum = psum.tile([P, S], F32, name="turned_sum%d" % t, tag=bank_tag)
+            for fetched, offsets in zip(pair, (n1_sb, n2_sb)):
+                for cols, lst in pieces:
+                    nc.scalar.activation(fetched[:, cols], window[:].indirect(offsets[:, lst]), ACT.Exp)
+            for b in range(PACK):
+                block = slice(b * P, (b + 1) * P)
+                for n in range(2):
+                    nc.tensor.matmul(
+                        turned_sum[:, block], pair[n][:, block], identity[:], start=(n == 0), stop=(n == 1), is_transpose=True
+                    )
+            pair_sum[t] = turned_sum[:]
 
-        log_sum = keep.tile([P, PACK, S], F32, name="log_sum", tag="half_y3")
+        scalar_gathers(2, "bank7", keep.tile([P, S], F32, name="half_y2"), halves(), [d_window[n][:, S:] for n in range(2)])
         logit = keep.tile([P, PACK, S], F32, name="logit")
+        logit_flat = logit[:].rearrange("p t j -> p (t j)")
+        d_plain = [logit[:, 2, :], logit[:, 3, :], logit_flat[:, HALF : HALF + S], keep.tile([P, S], F32, name="d_plain3")[:]]
         for t in range(PACK):
-            nc.scalar.activation(log_sum[:, t, :], pair_sum[:, t, :], ACT.Ln)
-            nc.vector.scalar_tensor_tensor(logit[:, t, :], y_bank[t][:], 0.5, log_sum[:, t, :], ALU.mult, ALU.subtract)
+            nc.scalar.copy(d_window[t][:, 0:S], d_bank[t][:])
+            nc.sync.dma_start(out=d_plain[t], in_=d_window[t][:, 0:S])
+        y_bank.append(psum.tile([P, S], F32, name="y3", tag="bank4"))
+        product(y_bank[3][:], w1_mx, 3, x_mx, slice(0, S))
+        scalar_gathers(3, "bank3", last_window, WHOLE, [keep.tile([P, S], F32, name="ex_n%d_3" % n)[:] for n in (1, 2)])
 
         w2_mx = quantise_weight(w2_raw, "w2")
 
+        h_window = [keep.tile([P, 2 * S], F32, name="h_window0", tag="w_bf", align_bytes=64)]
+        h_window += [keep.tile([P, 2 * S], F32, name="h_window%d" % t) for t in range(1, PACK)]
+        d_sums = [h_window[t][:, S:] for t in range(PACK)]
+
+        def gather_d(t):
+            nc.vector.tensor_tensor(d_sums[t], d_window[t][:].indirect(n4_sb[:]), d_plain[t], ALU.add)
+
+        for t in range(PACK - 1):
+            gather_d(t)
+
+        log_sum = [last_window[:, (t + 1) * S : (t + 2) * S] for t in range(3)]
+        log_sum.append(keep.tile([P, S], F32, name="log_sum3")[:])
+        back_bank = {3: "bank5", 2: "bank2"}
+        for t in (2, 3, 0, 1):
+            nc.scalar.activation(log_sum[t], pair_sum[t], ACT.Ln)
+            if t in VECTOR_PLANES:
+                nc.vector.scalar_tensor_tensor(logit[:, t, :], y_bank[t][:], 0.5, log_sum[t], ALU.mult, ALU.subtract)
+            else:
+                turned_back = psum.tile([P, S], F32, name="turned_back%d" % t, tag=back_bank[t])
+                for b in range(PACK):
+                    block = slice(b * P, (b + 1) * P)
+                    nc.tensor.transpose(turned_back[:, block], log_sum[t][:, block], identity[:])
+                nc.vector.tensor_tensor(logit[:, t, :], half_y[t], turned_back[:], ALU.subtract)
+
+        gate = [pair_sum[1]] + [logit[:, t, :] for t in range(1, PACK)]
+        nc.scalar.activation(gate[0][:, 0:LEAD], d_sums[0][:, 0:LEAD], ACT.Sigmoid)
+
         z_mx = mx_tiles("z")
-        h_bank = [psum.tile([P, S], F32, name="dh_bank%d" % t) for t in range(PACK)]
-        for c in range(S // CHUNK):
+        h_half = {}
+        for t, tags in ((0, ("bank7", "bank0")), (1, ("bank3", "bank1"))):
+            for u in range(2):
+                h_half[t, u] = psum.tile([P, HALF], F32, name="h%d_%d" % (t, u), tag=tags[u])[:]
+        for t, tag in ((2, "bank6"), (3, "bank4")):
+            whole = psum.tile([P, S], F32, name="h%d" % t, tag=tag)
+            for u in range(2):
+                h_half[t, u] = whole[:, u * HALF : (u + 1) * HALF]
+        chunks = S // CHUNK
+        z_bf = []
+
+        def make_z(c):
             cols = slice(c * CHUNK, (c + 1) * CHUNK)
-            share = keep.tile([P, CHUNK, PACK], F32, name="share%d" % c)
+            if c < chunks - 1:
+                share = keep.tile([P, CHUNK, PACK], F32, name="share%d" % c)[:]
+            else:
+                share = d_sums[3].rearrange("p (j t) -> p j t", t=PACK)
             nc.scalar.activation(
-                share[:].rearrange("p (a b) t -> p a t b", b=2),
+                share.rearrange("p (a b) t -> p a t b", b=2),
                 logit[:, :, cols].rearrange("p t (a b) -> p a t b", b=2),
                 ACT.Sigmoid,
             )
-            z_bf = keep.tile([P, CHUNK, PACK], BF16, name="z_bf%d" % c, align_bytes=64)
+            z_bf.append(keep.tile([P, CHUNK, PACK], BF16, name="z_bf%d" % c, align_bytes=64))
             nc.vector.scalar_tensor_tensor(
-                z_bf[:], share[:], 2.0, gain[:].unsqueeze(1).to_broadcast([P, CHUNK, PACK]), ALU.mult, ALU.mult
+                z_bf[c][:], share, 2.0, gain[:].unsqueeze(1).to_broadcast([P, CHUNK, PACK]), ALU.mult, ALU.mult
             )
+
+        def multiply_z(c):
+            cols = slice(c * CHUNK, (c + 1) * CHUNK)
             nc.vector.quantize_mx(
-                out=z_mx[0][:, cols].bitcast(FP8X4), scales=z_mx[1][:, cols], in_=z_bf[:].rearrange("p j t -> p (j t)")
+                out=z_mx[0][:, cols].bitcast(FP8X4), scales=z_mx[1][:, cols], in_=z_bf[c][:].rearrange("p j t -> p (j t)")
             )
             for t in range(PACK):
-                product(h_bank[t], w2_mx, t, z_mx, cols)
+                product(h_half[t, c // 2][:, (c % 2) * CHUNK : (c % 2 + 1) * CHUNK], w2_mx, t, z_mx, cols)
 
-        gate = keep.tile([P, PACK, S], F32, name="gate", tag="pair_sum")
-        late_sums = keep.tile([P, 2, S], F32, name="late_sums", tag="half_y3")
-        d_sums = [
-            keep.tile([P, S], F32, name="d_sum0", tag="ex_n1_3")[:],
-            keep.tile([P, S], F32, name="d_sum1", tag="ex_n2_3")[:],
-            late_sums[:, 0, :],
-            late_sums[:, 1, :],
-        ]
-        for t in range(PACK):
-            d_sum = d_sums[t]
-            for cols, lst in halves():
-                nc.vector.tensor_tensor(d_sum[:, cols], d_window[t][:].indirect(n4_sb[:, lst]), d_plain[t][:, cols], ALU.add)
-            nc.scalar.activation(gate[:, t, :], d_sum, ACT.Sigmoid)
+        make_z(0)
+        for c in range(1, chunks):
+            make_z(c)
+            multiply_z(c - 1)
+        multiply_z(chunks - 1)
+        gather_d(3)
 
         out_rows = out.rearrange("(q t r) j -> t q r j", t=PACK, r=2)
-        for t in range(PACK):
-            window = keep.tile([P, S], F32, name="h_window%d" % t)
-            nc.scalar.copy(window[:], h_bank[t][:])
+        h_sum = [keep.tile([P, S], F32, name="h_sum%d" % t) for t in range(PACK)]
+
+        def gather_h(t, pieces):
             plain = keep.tile([P, S], F32, name="h_plain%d" % t)
-            h_sum = keep.tile([P, S], F32, name="h_sum%d" % t)
+            for u, (cols, lst) in enumerate(halves()):
+                nc.scalar.copy(h_window[t][:, cols], h_half[t, u])
+                nc.scalar.copy(plain[:, cols], h_half[t, u])
+            for cols, lst in pieces:
+                nc.vector.tensor_tensor(h_sum[t][:, cols], h_window[t][:].indirect(n3_sb[:, lst]), plain[:, cols], ALU.add)
+            rest = slice(LEAD if t == 0 else 0, S)
+            nc.scalar.activation(gate[t][:, rest], d_sums[t][:, rest], ACT.Sigmoid)
+
+        def finish(t, pieces):
             result = keep.tile([P, S], F32, name="result%d" % t)
-            for cols, lst in halves():
-                nc.scalar.copy(plain[:, cols], h_bank[t][:, cols])
-                nc.vector.tensor_tensor(h_sum[:, cols], window[:].indirect(n3_sb[:, lst]), plain[:, cols], ALU.add)
-            for cols, lst in halves():
-                nc.vector.tensor_tensor(result[:, cols], h_sum[:, cols], gate[:, t, cols], ALU.mult)
+            for cols, lst in pieces:
+                nc.vector.tensor_tensor(result[:, cols], h_sum[t][:, cols], gate[t][:, cols], ALU.mult)
                 nc.sync.dma_start(out=out_rows[t][:, :, cols], in_=result[:, cols])
+
+        gather_h(0, halves())
+        gather_h(1, WHOLE)
+        finish(0, WHOLE)
+        gather_h(2, WHOLE)
+        finish(1, WHOLE)
+        gather_h(3, halves())
+        finish(2, WHOLE)
+        finish(3, halves())

@@ -159,33 +159,33 @@ def tile_picked_latetriebshare_none_p_kernel(
             for cols, lst in halves():
                 nc.vector.tensor_tensor(pair_sum[t][:, cols], ex[t][:].indirect(n2_sb[:, lst]), first[:, cols], ALU.add)
 
-        half_y = {}
-
-        def scalar_gathers(t, bank_tag, window, pieces, pair):
-            half_y[t] = window[:, 0:S]
-            nc.scalar.activation(half_y[t], y_bank[t][:], ACT.Copy, scale=0.5)
-            turned_sum = psum.tile([P, S], F32, name="turned_sum%d" % t, tag=bank_tag)
+        def scalar_gathers(t, window, pieces, pair):
+            nc.scalar.activation(window[:, 0:S], y_bank[t][:], ACT.Copy, scale=0.5)
             for fetched, offsets in zip(pair, (n1_sb, n2_sb)):
                 for cols, lst in pieces:
                     nc.scalar.activation(fetched[:, cols], window[:].indirect(offsets[:, lst]), ACT.Exp)
-            for b in range(PACK):
-                block = slice(b * P, (b + 1) * P)
-                for n in range(2):
-                    nc.tensor.matmul(
-                        turned_sum[:, block], pair[n][:, block], identity[:], start=(n == 0), stop=(n == 1), is_transpose=True
-                    )
-            pair_sum[t] = turned_sum[:]
 
-        scalar_gathers(2, "bank7", keep.tile([P, S], F32, name="half_y2"), halves(), [d_window[n][:, S:] for n in range(2)])
+        half_y2 = keep.tile([P, S], F32, name="half_y2")
+        pair2 = [d_window[n][:, S:] for n in range(2)]
+        scalar_gathers(2, half_y2, halves(), pair2)
         logit = keep.tile([P, PACK, S], F32, name="logit")
-        logit_flat = logit[:].rearrange("p t j -> p (t j)")
-        d_plain = [logit[:, 2, :], logit[:, 3, :], logit_flat[:, HALF : HALF + S], keep.tile([P, S], F32, name="d_plain3")[:]]
+        d_plain = [keep.tile([P, 2, HALF], F32, name="d_plain%d" % t)[:] for t in (0, 1, 3)]
+        d_plain.insert(2, logit[:].rearrange("p (a b) j -> p a (b j)", a=2)[:, :, S - HALF // 2 : S + HALF // 2])
         for t in range(PACK):
             nc.scalar.copy(d_window[t][:, 0:S], d_bank[t][:])
-            nc.sync.dma_start(out=d_plain[t], in_=d_window[t][:, 0:S])
+            nc.sync.dma_start(out=d_plain[t], in_=d_window[t][:, 0:S].rearrange("p (u c) -> p u c", u=2))
         y_bank.append(psum.tile([P, S], F32, name="y3", tag="bank4"))
         product(y_bank[3][:], w1_mx, 3, x_mx, slice(0, S))
-        scalar_gathers(3, "bank3", last_window, WHOLE, [keep.tile([P, S], F32, name="ex_n%d_3" % n)[:] for n in (1, 2)])
+        turned_sum = psum.tile([P, S], F32, name="turned_sum", tag="bank5")
+        for b in range(PACK):
+            block = slice(b * P, (b + 1) * P)
+            for n in range(2):
+                nc.tensor.matmul(
+                    turned_sum[:, block], pair2[n][:, block], identity[:], start=(n == 0), stop=(n == 1), is_transpose=True
+                )
+        pair_sum[2] = turned_sum[:]
+        pair3 = [keep.tile([P, S], F32, name="ex_n%d_3" % n)[:] for n in (1, 2)]
+        scalar_gathers(3, last_window, WHOLE, pair3)
 
         w2_mx = quantise_weight(w2_raw, "w2")
 
@@ -194,34 +194,41 @@ def tile_picked_latetriebshare_none_p_kernel(
         d_sums = [h_window[t][:, S:] for t in range(PACK)]
 
         def gather_d(t):
-            nc.vector.tensor_tensor(d_sums[t], d_window[t][:].indirect(n4_sb[:]), d_plain[t], ALU.add)
+            if t == 2:
+                for u, (cols, lst) in enumerate(halves()):
+                    nc.vector.tensor_tensor(d_sums[t][:, cols], d_window[t][:].indirect(n4_sb[:, lst]), d_plain[t][:, u, :], ALU.add)
+            else:
+                plain = d_plain[t].rearrange("p u c -> p (u c)")
+                nc.vector.tensor_tensor(d_sums[t], d_window[t][:].indirect(n4_sb[:]), plain, ALU.add)
 
-        for t in range(PACK - 1):
-            gather_d(t)
+        gather_d(0)
+        pair_sum[3] = d_plain[0].rearrange("p u c -> p (u c)")
+        nc.vector.tensor_tensor(pair_sum[3], pair3[0], pair3[1], ALU.add)
+        gather_d(1)
+        gather_d(2)
 
         log_sum = [last_window[:, (t + 1) * S : (t + 2) * S] for t in range(3)]
         log_sum.append(keep.tile([P, S], F32, name="log_sum3")[:])
-        back_bank = {3: "bank5", 2: "bank2"}
-        for t in (2, 3, 0, 1):
+        for t in (2, 0, 1, 3):
             nc.scalar.activation(log_sum[t], pair_sum[t], ACT.Ln)
-            if t in VECTOR_PLANES:
+            if t != 2:
                 nc.vector.scalar_tensor_tensor(logit[:, t, :], y_bank[t][:], 0.5, log_sum[t], ALU.mult, ALU.subtract)
             else:
-                turned_back = psum.tile([P, S], F32, name="turned_back%d" % t, tag=back_bank[t])
+                turned_back = psum.tile([P, S], F32, name="turned_back%d" % t, tag="bank2")
                 for b in range(PACK):
                     block = slice(b * P, (b + 1) * P)
                     nc.tensor.transpose(turned_back[:, block], log_sum[t][:, block], identity[:])
-                nc.vector.tensor_tensor(logit[:, t, :], half_y[t], turned_back[:], ALU.subtract)
+                nc.vector.tensor_tensor(logit[:, t, :], half_y2[:], turned_back[:], ALU.subtract)
 
-        gate = [pair_sum[1]] + [logit[:, t, :] for t in range(1, PACK)]
+        gate = [pair_sum[3]] + [logit[:, t, :] for t in range(1, PACK)]
         nc.scalar.activation(gate[0][:, 0:LEAD], d_sums[0][:, 0:LEAD], ACT.Sigmoid)
 
         z_mx = mx_tiles("z")
         h_half = {}
-        for t, tags in ((0, ("bank7", "bank0")), (1, ("bank3", "bank1"))):
+        for t, tags in ((0, ("bank5", "bank0")), (1, ("bank3", "bank1"))):
             for u in range(2):
                 h_half[t, u] = psum.tile([P, HALF], F32, name="h%d_%d" % (t, u), tag=tags[u])[:]
-        for t, tag in ((2, "bank6"), (3, "bank4")):
+        for t, tag in ((2, "bank6"), (3, "bank7")):
             whole = psum.tile([P, S], F32, name="h%d" % t, tag=tag)
             for u in range(2):
                 h_half[t, u] = whole[:, u * HALF : (u + 1) * HALF]

@@ -169,8 +169,10 @@ def tile_picked_latetriebshare_none_p_kernel(
         pair2 = [d_window[n][:, S:] for n in range(2)]
         scalar_gathers(2, half_y2, halves(), pair2)
         logit = keep.tile([P, PACK, S], F32, name="logit")
-        d_plain = [keep.tile([P, 2, HALF], F32, name="d_plain%d" % t)[:] for t in (0, 1, 3)]
-        d_plain.insert(2, logit[:].rearrange("p (a b) j -> p a (b j)", a=2)[:, :, S - HALF // 2 : S + HALF // 2])
+        d_plain = [
+            keep.tile([P, 2, HALF], F32, name="d_plain%d" % t, tag="d_plain%d" % t, align_bytes=64)[:] for t in (0, 2, 3)
+        ]
+        d_plain.insert(1, logit[:].rearrange("p (a b) j -> p a (b j)", a=2)[:, :, S - HALF // 2 : S + HALF // 2])
         for t in range(PACK):
             nc.scalar.copy(d_window[t][:, 0:S], d_bank[t][:])
             nc.sync.dma_start(out=d_plain[t], in_=d_window[t][:, 0:S].rearrange("p (u c) -> p u c", u=2))
@@ -194,7 +196,7 @@ def tile_picked_latetriebshare_none_p_kernel(
         d_sums = [h_window[t][:, S:] for t in range(PACK)]
 
         def gather_d(t):
-            if t == 2:
+            if t == 1:
                 for u, (cols, lst) in enumerate(halves()):
                     nc.vector.tensor_tensor(d_sums[t][:, cols], d_window[t][:].indirect(n4_sb[:, lst]), d_plain[t][:, u, :], ALU.add)
             else:
@@ -205,10 +207,9 @@ def tile_picked_latetriebshare_none_p_kernel(
         pair_sum[3] = d_plain[0].rearrange("p u c -> p (u c)")
         nc.vector.tensor_tensor(pair_sum[3], pair3[0], pair3[1], ALU.add)
         gather_d(1)
-        gather_d(2)
 
         log_sum = [last_window[:, (t + 1) * S : (t + 2) * S] for t in range(3)]
-        log_sum.append(keep.tile([P, S], F32, name="log_sum3")[:])
+        log_sum.append(d_sums[2])
         for t in (2, 0, 1, 3):
             nc.scalar.activation(log_sum[t], pair_sum[t], ACT.Ln)
             if t != 2:
@@ -220,6 +221,7 @@ def tile_picked_latetriebshare_none_p_kernel(
                     nc.tensor.transpose(turned_back[:, block], log_sum[t][:, block], identity[:])
                 nc.vector.tensor_tensor(logit[:, t, :], half_y2[:], turned_back[:], ALU.subtract)
 
+        gather_d(2)
         gate = [pair_sum[3]] + [logit[:, t, :] for t in range(1, PACK)]
         nc.scalar.activation(gate[0][:, 0:LEAD], d_sums[0][:, 0:LEAD], ACT.Sigmoid)
 
@@ -246,7 +248,8 @@ def tile_picked_latetriebshare_none_p_kernel(
                 logit[:, :, cols].rearrange("p t (a b) -> p a t b", b=2),
                 ACT.Sigmoid,
             )
-            z_bf.append(keep.tile([P, CHUNK, PACK], BF16, name="z_bf%d" % c, align_bytes=64))
+            tag = "d_plain2" if c == 0 else "z_bf%d" % c
+            z_bf.append(keep.tile([P, CHUNK, PACK], BF16, name="z_bf%d" % c, tag=tag, align_bytes=64))
             nc.vector.scalar_tensor_tensor(
                 z_bf[c][:], share, 2.0, gain[:].unsqueeze(1).to_broadcast([P, CHUNK, PACK]), ALU.mult, ALU.mult
             )
@@ -269,15 +272,18 @@ def tile_picked_latetriebshare_none_p_kernel(
         out_rows = out.rearrange("(q t r) j -> t q r j", t=PACK, r=2)
         h_sum = [keep.tile([P, S], F32, name="h_sum%d" % t) for t in range(PACK)]
 
-        def gather_h(t, pieces):
-            plain = keep.tile([P, S], F32, name="h_plain%d" % t)
+        h_plain = [keep.tile([P, S], F32, name="h_plain%d" % t) for t in range(PACK)]
+
+        def leave_banks(t):
             for u, (cols, lst) in enumerate(halves()):
                 nc.scalar.copy(h_window[t][:, cols], h_half[t, u])
-                nc.scalar.copy(plain[:, cols], h_half[t, u])
-            for cols, lst in pieces:
-                nc.vector.tensor_tensor(h_sum[t][:, cols], h_window[t][:].indirect(n3_sb[:, lst]), plain[:, cols], ALU.add)
+                nc.scalar.copy(h_plain[t][:, cols], h_half[t, u])
             rest = slice(LEAD if t == 0 else 0, S)
             nc.scalar.activation(gate[t][:, rest], d_sums[t][:, rest], ACT.Sigmoid)
+
+        def gather_h(t, pieces):
+            for cols, lst in pieces:
+                nc.vector.tensor_tensor(h_sum[t][:, cols], h_window[t][:].indirect(n3_sb[:, lst]), h_plain[t][:, cols], ALU.add)
 
         def finish(t, pieces):
             result = keep.tile([P, S], F32, name="result%d" % t)
@@ -285,11 +291,14 @@ def tile_picked_latetriebshare_none_p_kernel(
                 nc.vector.tensor_tensor(result[:, cols], h_sum[t][:, cols], gate[t][:, cols], ALU.mult)
                 nc.sync.dma_start(out=out_rows[t][:, :, cols], in_=result[:, cols])
 
+        for t in range(PACK):
+            leave_banks(t)
         gather_h(0, halves())
         gather_h(1, WHOLE)
         finish(0, WHOLE)
         gather_h(2, WHOLE)
         finish(1, WHOLE)
-        gather_h(3, halves())
+        gather_h(3, halves()[:1])
         finish(2, WHOLE)
+        gather_h(3, halves()[1:])
         finish(3, halves())

from contextlib import ExitStack

import concourse.mybir as mybir
from concourse.masks import make_identity

K, T, S, N, H = 512, 2048, 512, 512, 512
FLOPS = 3 * 2 * 512 * 512 * 512

F32 = mybir.dt.float32
BF16 = mybir.dt.bfloat16
I32 = mybir.dt.int32
U32 = mybir.dt.uint32
U16 = mybir.dt.uint16
U8 = mybir.dt.uint8
FP8X4 = mybir.dt.float8_e4m3fn_x4
ACT = mybir.ActivationFunctionType
ALU = mybir.AluOpType

P = 128
PACK = 4
HALF = S // 2
LIST_COLS = S // 16
CHUNK = 128
LEAD = 64
VECTOR_PLANES = (0, 1)
SCALAR_PLANES = (2, 3)


def halves():
    return [(slice(u * HALF, (u + 1) * HALF), slice(u * LIST_COLS // 2, (u + 1) * LIST_COLS // 2)) for u in range(2)]


WHOLE = [(slice(0, S), slice(0, LIST_COLS))]


def tile_picked_latetriebshare_none_p_kernel(
    tc, x_words, x_scales, w1, gn, w2, w3, offs, n1, n2, two, n3, n4, out
):
    nc = tc.nc
    with ExitStack() as ctx:
        keep = ctx.enter_context(tc.tile_pool(name="keep", bufs=1))
        psum = ctx.enter_context(tc.psum_pool(name="psum", bufs=1))

        def load_list(src, name):
            tile = keep.tile([P, LIST_COLS], U16, name=name)
            nc.sync.dma_start(tile[:], src)
            return tile

        def load_weight_half(w, u, name):
            raw = keep.tile([P, PACK, HALF], F32, name=name)
            nc.sync.dma_start(out=raw[:], in_=w.rearrange("(p j) c -> p j c", j=PACK)[:, :, u * HALF : (u + 1) * HALF])
            return raw[:]

        def dealt_views(grouped, raw, u, parts=2):
            dst = grouped[:].rearrange("p (t u q r j) -> p u q t j r", t=PACK, u=parts, r=2, j=PACK)[:, u]
            src = raw.rearrange("p j (q t r) -> p q t j r", t=PACK, r=2)
            return dst, src

        def mx_tiles(name, scale_tag=None):
            codes = keep.tile([P, 512], U32, name=name + "_codes", tag=name + "_codes", align_bytes=64)
            scales = keep.tile([P, 512], U8, name=name + "_scales", tag=scale_tag or name + "_scales", align_bytes=64)
            return codes, scales

        def product(result, w_mx, t, x_mx, cols):
            rows = slice(t * P, (t + 1) * P)
            nc.tensor.matmul_mx(
                out=result,
                lhsT=w_mx[0][:, rows].bitcast(FP8X4),
                lhsT_scale=w_mx[1][:, rows],
                rhs=x_mx[0][:, cols].bitcast(FP8X4),
                rhs_scale=x_mx[1][:, cols],
                start=True,
                stop=True,
            )

        scale_table = keep.tile([P, T], U8, name="scale_table", align_bytes=64)
        nc.gpsimd.memset(scale_table[:].bitcast(I32), 0)
        identity = keep.tile([P, P], F32, name="identity")
        make_identity(nc, identity[:])
        last_window = keep.tile([P, PACK * S], F32, name="last_window")
        nc.gpsimd.memset(last_window[:, S:], 0.0)
        offs_sb = load_list(offs, "offs_sb")
        two_sb = load_list(two, "two_sb")
        for q in range(4):
            nc.sync.dma_start(
                out=scale_table[32 * q : 32 * q + 4, :].bitcast(I32),
                in_=x_scales[0, 4 * q : 4 * q + 4, :].bitcast(I32),
            )
        word_table = keep.tile([P, T], I32, name="word_table", align_bytes=64)
        nc.sync.dma_start(out=word_table[:], in_=x_words[0].rearrange("p n t -> p (n t)").bitcast(I32))
        w1_raw = [load_weight_half(w1, u, "w1_raw%d" % u) for u in range(2)]
        n1_sb = load_list(n1, "n1_sb")
        n2_sb = load_list(n2, "n2_sb")
        w3_raw = [load_weight_half(w3, u, "w3_raw%d" % u) for u in range(2)]
        w2_rows = w2.rearrange("(q t r) c -> r q t c", t=PACK, r=2)
        w2_whole = keep.tile([P, PACK, N], F32, name="w2_raw")
        for r in range(2):
            nc.sync.dma_start(out=w2_whole[r:P:2], in_=w2_rows[r])
        w2_raw = [w2_whole[:]]
        n4_sb = load_list(n4, "n4_sb")
        n3_sb = load_list(n3, "n3_sb")
        gain = keep.tile([P, PACK], F32, name="gain")
        gn_rows = gn.rearrange("(q t r) o -> r q (t o)", t=PACK, r=2)
        with nc.allow_non_contiguous_dma(reason="one gain a feature"):
            for r in range(2):
                nc.sync.dma_start(out=gain[r:P:2], in_=gn_rows[r])

        x_mx, x_two_mx = mx_tiles("x_offs"), mx_tiles("x_two")
        for picked, offsets in ((x_mx, offs_sb), (x_two_mx, two_sb)):
            nc.vector.tensor_copy(picked[1][:], scale_table[:].indirect(offsets[:]))
        for picked, offsets in ((x_mx, offs_sb), (x_two_mx, two_sb)):
            nc.vector.tensor_copy(picked[0][:], word_table[:].bitcast(U32).indirect(offsets[:]))

        w1_bf = keep.tile([P, PACK * H], BF16, name="w1_bf", tag="w_bf", align_bytes=64)
        nc.scalar.copy(*dealt_views(w1_bf, w1_raw[0], 0))
        nc.vector.tensor_copy(*dealt_views(w1_bf, w1_raw[1], 1))
        w1_mx = mx_tiles("w1")
        y_bank = []
        for t in range(PACK):
            nc.vector.quantize_mx(
                out=w1_mx[0][:, t * P : (t + 1) * P].bitcast(FP8X4),
                scales=w1_mx[1][:, t * P : (t + 1) * P],
                in_=w1_bf[:, t * 512 : (t + 1) * 512],
            )
            if t < 3:
                bank = psum.tile([P, S], F32, name="y%d" % t, tag="bank%d" % t)
                product(bank[:], w1_mx, t, x_mx, slice(0, S))
                y_bank.append(bank)


        def quantise_weight(raw, name):
            grouped = keep.tile([P, PACK * 512], BF16, name=name + "_bf", tag="w_bf", align_bytes=64)
            for u in range(len(raw)):
                dst, src = dealt_views(grouped, raw[u], u, len(raw))
                nc.vector.tensor_copy(dst, src)
            w_mx = mx_tiles(name)
            nc.vector.quantize_mx(out=w_mx[0][:].bitcast(FP8X4), scales=w_mx[1][:], in_=grouped[:])
            return w_mx

        w3_mx = quantise_weight(w3_raw, "w3")
        d_bank = []
        for t in range(PACK):
            bank = psum.tile([P, S], F32, name="d%d" % t, tag="bank%d" % (3 + t))
            product(bank[:], w3_mx, t, x_two_mx, slice(0, S))
            d_bank.append(bank)

        d_window = [keep.tile([P, 2 * S], F32, name="d_window%d" % t) for t in range(PACK)]
        pair_sum = {}
        ex = {}
        for t in VECTOR_PLANES:
            ex[t] = keep.tile([P, S], F32, name="ex%d" % t)
            nc.scalar.activation(ex[t][:], y_bank[t][:], ACT.Exp, scale=0.5)
        firsts = keep.tile([P, len(VECTOR_PLANES), S], F32, name="ex_n1_vector", tag="w_bf", align_bytes=64)
        for t in VECTOR_PLANES:
            first = firsts[:, t, :]
            pair_sum[t] = d_window[2 + t][:, S:]
            for cols, lst in halves():
                nc.vector.tensor_copy(first[:, cols], ex[t][:].indirect(n1_sb[:, lst]))
            for cols, lst in halves():
                nc.vector.tensor_tensor(pair_sum[t][:, cols], ex[t][:].indirect(n2_sb[:, lst]), first[:, cols], ALU.add)

        def scalar_gathers(t, window, pieces, pair):
            nc.scalar.activation(window[:, 0:S], y_bank[t][:], ACT.Copy, scale=0.5)
            for fetched, offsets in zip(pair, (n1_sb, n2_sb)):
                for cols, lst in pieces:
                    nc.scalar.activation(fetched[:, cols], window[:].indirect(offsets[:, lst]), ACT.Exp)

        half_y2 = keep.tile([P, S], F32, name="half_y2")
        pair2 = [d_window[n][:, S:] for n in range(2)]
        scalar_gathers(2, half_y2, halves(), pair2)
        logit = keep.tile([P, PACK, S], F32, name="logit")
        d_plain = [
            keep.tile([P, 2, HALF], F32, name="d_plain%d" % t, tag="d_plain%d" % t, align_bytes=64)[:] for t in (0, 2, 3)
        ]
        d_plain.insert(1, logit[:].rearrange("p (a b) j -> p a (b j)", a=2)[:, :, S - HALF // 2 : S + HALF // 2])
        for t in range(PACK):
            nc.scalar.copy(d_window[t][:, 0:S], d_bank[t][:])
            nc.sync.dma_start(out=d_plain[t], in_=d_window[t][:, 0:S].rearrange("p (u c) -> p u c", u=2))
        y_bank.append(psum.tile([P, S], F32, name="y3", tag="bank4"))
        product(y_bank[3][:], w1_mx, 3, x_mx, slice(0, S))
        turned_sum = psum.tile([P, S], F32, name="turned_sum", tag="bank5")
        for b in range(PACK):
            block = slice(b * P, (b + 1) * P)
            for n in range(2):
                nc.tensor.matmul(
                    turned_sum[:, block], pair2[n][:, block], identity[:], start=(n == 0), stop=(n == 1), is_transpose=True
                )
        pair_sum[2] = turned_sum[:]
        pair3 = [keep.tile([P, S], F32, name="ex_n%d_3" % n)[:] for n in (1, 2)]
        scalar_gathers(3, last_window, WHOLE, pair3)

        w2_mx = quantise_weight(w2_raw, "w2")

        h_window = [keep.tile([P, 2 * S], F32, name="h_window0", tag="w_bf", align_bytes=64)]
        h_window += [keep.tile([P, 2 * S], F32, name="h_window%d" % t) for t in range(1, PACK)]
        d_sums = [h_window[t][:, S:] for t in range(PACK)]

        def gather_d(t):
            if t == 1:
                for u, (cols, lst) in enumerate(halves()):
                    nc.vector.tensor_tensor(d_sums[t][:, cols], d_window[t][:].indirect(n4_sb[:, lst]), d_plain[t][:, u, :], ALU.add)
            else:
                plain = d_plain[t].rearrange("p u c -> p (u c)")
                nc.vector.tensor_tensor(d_sums[t], d_window[t][:].indirect(n4_sb[:]), plain, ALU.add)

        gather_d(0)
        pair_sum[3] = d_plain[0].rearrange("p u c -> p (u c)")
        nc.vector.tensor_tensor(pair_sum[3], pair3[0], pair3[1], ALU.add)
        gather_d(1)

        log_sum = [last_window[:, (t + 1) * S : (t + 2) * S] for t in range(3)]
        log_sum.append(d_sums[2])
        for t in (2, 0, 1, 3):
            nc.scalar.activation(log_sum[t], pair_sum[t], ACT.Ln)
            if t != 2:
                nc.vector.scalar_tensor_tensor(logit[:, t, :], y_bank[t][:], 0.5, log_sum[t], ALU.mult, ALU.subtract)
            else:
                turned_back = psum.tile([P, S], F32, name="turned_back%d" % t, tag="bank2")
                for b in range(PACK):
                    block = slice(b * P, (b + 1) * P)
                    nc.tensor.transpose(turned_back[:, block], log_sum[t][:, block], identity[:])
                nc.vector.tensor_tensor(logit[:, t, :], half_y2[:], turned_back[:], ALU.subtract)

        gather_d(2)
        gate = [pair_sum[3]] + [logit[:, t, :] for t in range(1, PACK)]
        nc.scalar.activation(gate[0][:, 0:LEAD], d_sums[0][:, 0:LEAD], ACT.Sigmoid)

        z_mx = mx_tiles("z")
        h_half = {}
        for t, tags in ((0, ("bank5", "bank0")), (1, ("bank3", "bank1"))):
            for u in range(2):
                h_half[t, u] = psum.tile([P, HALF], F32, name="h%d_%d" % (t, u), tag=tags[u])[:]
        for t, tag in ((2, "bank6"), (3, "bank7")):
            whole = psum.tile([P, S], F32, name="h%d" % t, tag=tag)
            for u in range(2):
                h_half[t, u] = whole[:, u * HALF : (u + 1) * HALF]
        chunks = S // CHUNK
        z_bf = []

        def make_z(c):
            cols = slice(c * CHUNK, (c + 1) * CHUNK)
            if c < chunks - 1:
                share = keep.tile([P, CHUNK, PACK], F32, name="share%d" % c)[:]
            else:
                share = d_sums[3].rearrange("p (j t) -> p j t", t=PACK)
            nc.scalar.activation(
                share.rearrange("p (a b) t -> p a t b", b=2),
                logit[:, :, cols].rearrange("p t (a b) -> p a t b", b=2),
                ACT.Sigmoid,
            )
            tag = "d_plain2" if c == 0 else "z_bf%d" % c
            z_bf.append(keep.tile([P, CHUNK, PACK], BF16, name="z_bf%d" % c, tag=tag, align_bytes=64))
            nc.vector.scalar_tensor_tensor(
                z_bf[c][:], share, 2.0, gain[:].unsqueeze(1).to_broadcast([P, CHUNK, PACK]), ALU.mult, ALU.mult
            )

        def multiply_z(c):
            cols = slice(c * CHUNK, (c + 1) * CHUNK)
            nc.vector.quantize_mx(
                out=z_mx[0][:, cols].bitcast(FP8X4), scales=z_mx[1][:, cols], in_=z_bf[c][:].rearrange("p j t -> p (j t)")
            )
            for t in range(PACK):
                product(h_half[t, c // 2][:, (c % 2) * CHUNK : (c % 2 + 1) * CHUNK], w2_mx, t, z_mx, cols)

        make_z(0)
        for c in range(1, chunks):
            make_z(c)
            multiply_z(c - 1)
        multiply_z(chunks - 1)
        gather_d(3)

        out_rows = out.rearrange("(q t r) j -> t q r j", t=PACK, r=2)
        h_sum = [keep.tile([P, S], F32, name="h_sum%d" % t) for t in range(PACK)]

        h_plain = [keep.tile([P, S], F32, name="h_plain%d" % t) for t in range(PACK)]

        def leave_banks(t):
            for u, (cols, lst) in enumerate(halves()):
                nc.scalar.copy(h_window[t][:, cols], h_half[t, u])
                nc.scalar.copy(h_plain[t][:, cols], h_half[t, u])
            rest = slice(LEAD if t == 0 else 0, S)
            nc.scalar.activation(gate[t][:, rest], d_sums[t][:, rest], ACT.Sigmoid)

        def gather_h(t, pieces):
            for cols, lst in pieces:
                nc.vector.tensor_tensor(h_sum[t][:, cols], h_window[t][:].indirect(n3_sb[:, lst]), h_plain[t][:, cols], ALU.add)

        def finish(t, pieces):
            result = keep.tile([P, S], F32, name="result%d" % t)
            for cols, lst in pieces:
                nc.vector.tensor_tensor(result[:, cols], h_sum[t][:, cols], gate[t][:, cols], ALU.mult)
                nc.sync.dma_start(out=out_rows[t][:, :, cols], in_=result[:, cols])

        for t in range(PACK):
            leave_banks(t)
        gather_h(0, halves())
        gather_h(1, WHOLE)
        finish(0, WHOLE)
        gather_h(2, WHOLE)
        finish(1, WHOLE)
        gather_h(3, halves()[:1])
        finish(2, WHOLE)
        gather_h(3, halves()[1:])
        finish(3, halves())
